import numpy as np
import ml_dtypes


def mxq(x, axis, fmt="e4m3"):
    dtype, down = {"e4m3": (ml_dtypes.float8_e4m3fn, 7), "e5m2": (ml_dtypes.float8_e5m2, 14)}[fmt]
    v = np.moveaxis(np.asarray(x, np.float32).astype(ml_dtypes.bfloat16).astype(np.float64), axis, -1)
    blocks = v.reshape(v.shape[:-1] + (-1, 32))
    amax = np.abs(blocks).max(-1, keepdims=True)
    byte = np.maximum(np.where(amax > 0, np.frexp(amax)[1] - 1 + 127, 0) - down, 1)
    scale = np.exp2(byte - 127.0)
    codes = (blocks / scale).astype(np.float32).astype(dtype).astype(np.float64)
    return np.moveaxis((codes * scale).reshape(v.shape), -1, axis)


WIDE = False


def mx_kscale(k):
    if not WIDE:
        return np.ones(k)
    levels = np.array([10, -10, 5, -5, 0])
    if k % 512:
        return np.exp2(np.random.permutation(np.resize(levels, k // 32))).repeat(32)
    a = np.empty((k // 512, 16))
    for p in range(k // 512):
        a[p, :8] = np.random.permutation(np.resize(levels, 8))
        for g in range(8):
            far = levels[np.abs(levels - a[p, g]) >= 10]
            a[p, g + 8] = far[np.random.randint(len(far))]
    return np.exp2(a.ravel()).repeat(32)


def f64(x):
    return np.asarray(x).astype(np.float64)


def striped(idx):
    return np.tile(np.asarray(idx).reshape(-1, 16).T, (8, 1)).astype(np.uint16)


def unstriped(offs):
    return offs[:16].T.reshape(-1).astype(np.int64)


def striped8(idx):
    return np.asarray(idx).reshape(8, -1, 16).transpose(0, 2, 1).reshape(128, -1).astype(np.uint16)


def unstriped8(offs):
    return offs.reshape(8, 16, -1).transpose(0, 2, 1).reshape(8, -1).astype(np.int64)


def pick8(x, idx, run):
    r = np.arange(len(x))
    return x[r[:, None], idx[r % (8 * run) // run]]


E2M1 = np.array([0.0, 0.5, 1.0, 1.5, 2.0, 3.0, 4.0, 6.0, -0.0, -0.5, -1.0, -1.5, -2.0, -3.0, -4.0, -6.0])


def pack_weight(w, fmt):
    k, n = w.shape
    w = f64(np.asarray(w, np.float32).astype(ml_dtypes.bfloat16)).reshape(k // 32, 32, n)
    amax = np.abs(w).max(1)
    if fmt == "e4m3":
        byte = np.frexp(amax)[1] - 1 + 127 - 7
    else:
        mant, ex = np.frexp(amax / 6.0)
        byte = np.where(mant > 0.5, ex, ex - 1) + 127
    byte = np.clip(np.where(amax > 0, byte, 1), 1, 254)
    scaled = (w * np.exp2(127.0 - byte)[:, None, :]).reshape(k, n).astype(np.float32)
    by_word = np.ascontiguousarray(scaled.reshape(k // 512, 128, 4, n).transpose(0, 1, 3, 2))
    if fmt == "e4m3":
        words = by_word.astype(ml_dtypes.float8_e4m3fn).view(np.uint8)
    else:
        c = by_word.astype(ml_dtypes.float4_e2m1fn).view(np.uint8) & 0xF
        words = (c[..., 0::2] | (c[..., 1::2] << 4)).reshape(k // 512, 128, 2 * n)
    return np.ascontiguousarray(words), np.ascontiguousarray(byte.astype(np.uint8).reshape(k // 512, 16, n))


def unpack_weight(words, scales, fmt):
    g, _, n = scales.shape
    words = np.ascontiguousarray(words).reshape(g, 128, n, -1)
    if fmt == "e4m3":
        vals = words.view(ml_dtypes.float8_e4m3fn).astype(np.float64)
    else:
        nib = np.empty((g, 128, n, 4), np.uint8)
        nib[..., 0::2] = words & 0xF
        nib[..., 1::2] = words >> 4
        vals = E2M1[nib]
    vals = vals * np.repeat(np.exp2(scales.astype(np.float64) - 127.0), 8, axis=1)[..., None]
    return vals.transpose(0, 1, 3, 2).reshape(g * 512, n)


def sigmoid(v):
    return 1.0 / (1.0 + np.exp(-v))


def bf(x):
    return np.asarray(x, np.float32).astype(ml_dtypes.bfloat16)


def planes(Y):
    r, m = Y.shape
    b = f64(bf(Y)).reshape(r // 32, 32, m)
    amax = np.abs(b).max(1)
    byte = np.clip(np.where(amax > 0, np.frexp(amax)[1] - 1 + 127 - 7, 1), 1, 254)
    codes = (b * np.exp2(127.0 - byte)[:, None, :]).reshape(r, m).astype(np.float32).astype(ml_dtypes.float8_e4m3fn).view(np.uint8)
    words = codes.reshape(r // 512, 128, 4, m).transpose(0, 1, 3, 2)
    return np.ascontiguousarray(words), np.ascontiguousarray(byte.astype(np.uint8).reshape(r // 512, 16, m))


K, R, F, T, J, M = 512, 512, 512, 2048, 512, 128


def setup_inputs():
    n = np.random.standard_normal
    idx = np.random.permutation(T)[:J]
    idx2 = np.stack([np.random.permutation(J)[:M] for _ in range(8)])
    idx3 = np.stack([np.random.permutation(J)[:M] for _ in range(8)])
    fk = mx_kscale(K)
    fr = mx_kscale(R)
    tabp = pack_weight(n((K, T)) / fk[:, None], "e2m1")
    return {
        "tab_words": tabp[0],
        "tab_scales": tabp[1],
        "w1": (n((K, R)) * 1 / np.sqrt(K) * fk[:, None]).astype(np.float32),
        "dw1": (n((K, R)) * 1 / np.sqrt(K) * fk[:, None]).astype(np.float32),
        "gain": (np.random.uniform(0.5, 1.5, (R, 1))).astype(np.float32),
        "rs": (np.random.uniform(0.5, 2.0, (R, 1)) * fr[:, None]).astype(np.float32),
        "wor": (n((R, F)) * 1 / np.sqrt(R) / fr[:, None]).astype(np.float32),
        "res": (n((F, M)) * 0.5).astype(np.float32),
        "offs": striped(idx),
        "offs2": striped8(idx2),
        "offs3": striped8(idx3),
    }


def reference(tab_words, tab_scales, w1, dw1, gain, rs, wor, res, offs, offs2, offs3):
    idx = unstriped(offs)
    idx2 = unstriped8(offs2)
    idx3 = unstriped8(offs3)
    tabu = unpack_weight(tab_words, tab_scales, "e2m1")
    w1q = mxq(f64(w1), 0, "e4m3")
    tabidxg = tabu[:, idx]
    a = w1q.T @ tabidxg
    dw1q = mxq(f64(dw1), 0, "e4m3")
    ta = dw1q.T @ tabidxg
    h1 = a * f64(gain)
    th1 = ta * f64(gain)
    tu1 = pick8(th1, idx2, 64) * (1.0 - np.square(np.tanh(pick8(h1, idx2, 64)))) * sigmoid(pick8(h1, idx3, 64)) + pick8(th1, idx3, 64) * sigmoid(pick8(h1, idx3, 64)) * (1.0 - sigmoid(pick8(h1, idx3, 64))) * np.tanh(pick8(h1, idx2, 64))
    fo1 = tu1 * f64(rs)
    worq = mxq(f64(wor), 0, "e4m3")
    fo1q = mxq(fo1, 0, "e4m3")
    yo = worq.T @ fo1q
    y = yo + f64(res)
    words, scales = planes(y)
    return y, words, scales

@@ -1,0 +1,163 @@
+from contextlib import ExitStack
+
+import concourse.mybir as mybir
+
+K, R, F, T, J, M = 512, 512, 512, 2048, 512, 128
+FLOPS = 2 * K * R * J * 2 + 2 * R * F * M
+
+F32 = mybir.dt.float32
+BF16 = mybir.dt.bfloat16
+I32 = mybir.dt.int32
+U32 = mybir.dt.uint32
+U16 = mybir.dt.uint16
+U8 = mybir.dt.uint8
+FP8X4 = mybir.dt.float8_e4m3fn_x4
+FP4X4 = mybir.dt.float4_e2m1fn_x4
+ALU = mybir.AluOpType
+ACT = mybir.ActivationFunctionType
+
+P = 128
+PACK = 4
+HALF = 256
+
+
+def deal(copy, grouped, raw, c0):
+    m0, n = c0 // PACK, raw.shape[2] // PACK
+    copy(
+        grouped[:, :, m0 : m0 + n, :].rearrange("p t m j -> p m j t"),
+        raw.rearrange("p j (m t) -> p m j t", t=PACK),
+    )
+
+
+def tile_attend_tcweights_o_pl_kernel(tc, tab_words, tab_scales, w1, dw1, gain, rs, wor, res, offs, offs2, offs3, out_0, out_1, out_2):
+    nc = tc.nc
+    with ExitStack() as ctx:
+        keep = ctx.enter_context(tc.tile_pool(name="keep", bufs=1))
+        psum = ctx.enter_context(tc.psum_pool(name="psum", bufs=1))
+
+        def sb(name, shape, dtype):
+            return keep.tile(shape, dtype, name=name, align_bytes=64)
+
+        list1, list2, list3 = sb("list1", [P, J // 16], U16), sb("list2", [P, M // 16], U16), sb("list3", [P, M // 16], U16)
+        words_all, bytes_all = sb("words_all", [P, T], U16), sb("bytes_all", [P, T], U8)
+        warm_in, warm_out = sb("warm_in", [P, 1], F32), sb("warm_out", [P, 1], F32)
+        nc.vector.memset(bytes_all[:].bitcast(I32), 0)
+        nc.gpsimd.memset(warm_in[:], 0.0)
+        nc.scalar.activation(warm_out[:], warm_in[:], ACT.Sigmoid)
+
+        def load_half(name, w, i):
+            half = sb("%s_raw%d" % (name, i), [P, PACK, HALF], F32)
+            nc.sync.dma_start(half[:], w.rearrange("(p j) c -> p j c", j=PACK)[:, :, i * HALF : (i + 1) * HALF])
+            return half
+
+        gain_sb, rs_sb = sb("gain_sb", [P, PACK], F32), sb("rs_sb", [P, PACK], F32)
+        nc.sync.dma_start(list1[:], offs)
+        nc.sync.dma_start(words_all[:].bitcast(I32), tab_words[0].bitcast(I32))
+        w1_raw = [load_half("w1", w1, 0)]
+        nc.sync.dma_start(list3[:], offs3)
+        for q in range(4):
+            nc.sync.dma_start(bytes_all[32 * q : 32 * q + 4, :].bitcast(I32), tab_scales[0, 4 * q : 4 * q + 4, :].bitcast(I32))
+        w1_raw.append(load_half("w1", w1, 1))
+        dw1_raw = [load_half("dw1", dw1, 0)]
+        nc.sync.dma_start(gain_sb[:], gain.rearrange("(p t) o -> p (t o)", t=PACK))
+        nc.sync.dma_start(list2[:], offs2)
+        dw1_raw.append(load_half("dw1", dw1, 1))
+        wor_raw = sb("wor_raw", [P, PACK, F], F32)
+        nc.sync.dma_start(wor_raw[:], wor.rearrange("(p j) c -> p j c", j=PACK))
+        nc.sync.dma_start(rs_sb[:], rs.rearrange("(p t) o -> p (t o)", t=PACK))
+        res_sb = sb("res_sb", [P, PACK, M], F32)
+        nc.sync.dma_start(res_sb[:], res.rearrange("(p t) m -> p t m", t=PACK))
+
+        tab_w, tab_s = sb("tab_w", [P, J], U16), sb("tab_s", [P, J], U8)
+        nc.vector.tensor_copy(tab_w[:], words_all[:].indirect(list1[:]))
+        nc.vector.tensor_copy(tab_s[:], bytes_all[:].indirect(list1[:]))
+
+        def operand(name):
+            return sb(name + "_bf", [P, PACK, P, PACK], BF16), sb(name + "_c", [P, PACK, P], U32), sb(name + "_s", [P, PACK, P], U8)
+
+        def quantise(op, t0, t1):
+            grouped, codes, scales = op
+            nc.vector.quantize_mx(
+                out=codes[:, t0:t1, :].rearrange("p t m -> p (t m)").bitcast(FP8X4),
+                scales=scales[:, t0:t1, :].rearrange("p t m -> p (t m)"),
+                in_=grouped[:, t0:t1, :, :].rearrange("p t m j -> p (t m j)"),
+            )
+
+        def first_layer(op, bank, t):
+            nc.tensor.matmul_mx(
+                out=bank[:], lhsT=op[1][:, t, :].bitcast(FP8X4), lhsT_scale=op[2][:, t, :],
+                rhs=tab_w[:].bitcast(FP4X4), rhs_scale=tab_s[:], start=True, stop=True,
+            )
+
+        w1q, dw1q, worq = operand("w1"), operand("dw1"), operand("wor")
+        a_bank = [psum.tile([P, J], F32, name="a%d" % t) for t in range(PACK)]
+        ta_bank = [psum.tile([P, J], F32, name="ta%d" % t) for t in range(PACK)]
+        h1 = [sb("h1_%d" % t, [P, J], F32) for t in range(PACK)]
+        th1 = [sb("th1_%d" % t, [P, J], F32) for t in range(PACK)]
+        s2, s3, tsq, s3r, wb, pa, pb = [sb(n, [P, PACK, M], F32) for n in ("s2", "s3", "tsq", "s3r", "wb", "pa", "pb")]
+
+        deal(nc.scalar.copy, w1q[0], w1_raw[0][:], 0)
+        deal(nc.vector.tensor_copy, w1q[0], w1_raw[1][:], HALF)
+        for t0, t1 in ((0, 1), (1, 2), (2, 4)):
+            quantise(w1q, t0, t1)
+        for t in range(PACK):
+            first_layer(w1q, a_bank[t], t)
+        for i in range(2):
+            deal(nc.vector.tensor_copy, dw1q[0], dw1_raw[i][:], i * HALF)
+        for t0, t1 in ((0, 1), (1, 2), (2, 4)):
+            quantise(dw1q, t0, t1)
+        for t in range(PACK):
+            first_layer(dw1q, ta_bank[t], t)
+
+        for t in (0, 1):
+            nc.vector.tensor_scalar_mul(th1[t][:], ta_bank[t][:], gain_sb[:, t : t + 1])
+        deal(nc.vector.tensor_copy, worq[0], wor_raw[:], 0)
+        quantise(worq, 0, PACK)
+        n3r, wa = sb("wor_raw", [P, PACK, M], F32), sb("wor_bf", [P, PACK, M], F32)
+
+        for t0 in (0, 2):
+            pair = slice(t0, t0 + 2)
+            for t in (t0, t0 + 1):
+                nc.scalar.activation(h1[t][:], a_bank[t][:], ACT.Copy, scale=gain_sb[:, t : t + 1])
+            for t in (t0, t0 + 1):
+                nc.scalar.activation(s3[:, t, :], h1[t][:].indirect(list3[:]), ACT.Sigmoid)
+                nc.scalar.activation(s2[:, t, :], h1[t][:].indirect(list2[:]), ACT.Sigmoid, scale=2.0)
+            for t in (t0, t0 + 1):
+                nc.scalar.activation(s3r[:, t, :], s3[:, t, :], ACT.Copy, scale=rs_sb[:, t : t + 1])
+            nc.scalar.activation(tsq[:, pair, :], s2[:, pair, :], ACT.Square, scale=2.0, bias=-1.0)
+            for t in (t0, t0 + 1):
+                if t > 1:
+                    nc.scalar.activation(th1[t][:], ta_bank[t][:], ACT.Copy, scale=gain_sb[:, t : t + 1])
+            nc.vector.scalar_tensor_tensor(n3r[:, pair, :], s3[:, pair, :], 1.0, s3r[:, pair, :], ALU.subtract, ALU.mult)
+            nc.vector.scalar_tensor_tensor(wa[:, pair, :], tsq[:, pair, :], 1.0, s3r[:, pair, :], ALU.subtract, ALU.mult)
+            nc.vector.scalar_tensor_tensor(wb[:, pair, :], s2[:, pair, :], 0.5, n3r[:, pair, :], ALU.subtract, ALU.mult)
+            for t in (t0, t0 + 1):
+                nc.vector.tensor_tensor(pa[:, t, :], th1[t][:].indirect(list2[:]), wa[:, t, :], ALU.mult)
+                nc.vector.tensor_tensor(pb[:, t, :], th1[t][:].indirect(list3[:]), wb[:, t, :], ALU.mult)
+
+        fo_bf, fo_c, fo_s = sb("fo_bf", [P, M, PACK], BF16), sb("fo_c", [P, M], U32), sb("fo_s", [P, M], U8)
+        nc.vector.scalar_tensor_tensor(
+            fo_bf[:], pb[:].rearrange("p t m -> p m t"), -2.0, pa[:].rearrange("p t m -> p m t"), ALU.mult, ALU.subtract
+        )
+        nc.vector.quantize_mx(out=fo_c[:].bitcast(FP8X4), scales=fo_s[:], in_=fo_bf[:].rearrange("p m t -> p (m t)"))
+
+        y, y_bf = sb("y", [P, PACK, M], F32), sb("y_bf", [P, M, PACK], BF16)
+        y_c, y_s = sb("y_c", [P, M], U32), sb("y_s", [P, M], U8)
+        out_rows = out_0.rearrange("(p t) m -> p t m", t=PACK)
+        for i in range(2):
+            pair = slice(2 * i, 2 * i + 2)
+            yo = psum.tile([P, 2, M], F32, name="a%d" % i)
+            for u in range(2):
+                t = 2 * i + u
+                nc.tensor.matmul_mx(
+                    out=yo[:, u, :], lhsT=worq[1][:, t, :].bitcast(FP8X4), lhsT_scale=worq[2][:, t, :],
+                    rhs=fo_c[:].bitcast(FP8X4), rhs_scale=fo_s[:], start=True, stop=True,
+                )
+            nc.vector.tensor_tensor(y[:, pair, :], yo[:], res_sb[:, pair, :], ALU.add)
+            nc.sync.dma_start(out_rows[:, pair, :], y[:, pair, :])
+        nc.vector.tensor_copy(y_bf[:].rearrange("p (c i) t -> p c t i", i=4), y[:].rearrange("p t (c i) -> p c t i", i=4))
+        nc.vector.quantize_mx(out=y_c[:].bitcast(FP8X4), scales=y_s[:], in_=y_bf[:].rearrange("p m t -> p (m t)"))
+        nc.scalar.dma_start(out_1[0].rearrange("p c r -> p (c r)").bitcast(I32), y_c[:].bitcast(I32))
+        for q in range(4):
+            queue = nc.sync if q % 2 == 0 else nc.scalar
+            queue.dma_start(out_2[0, 4 * q : 4 * q + 4, :].bitcast(I32), y_s[32 * q : 32 * q + 4, :].bitcast(I32))

@@ -1,3 +1,4 @@
+import math
 from contextlib import ExitStack
 
 import concourse.mybir as mybir
@@ -18,14 +19,12 @@ ACT = mybir.ActivationFunctionType
 
 P = 128
 PACK = 4
-HALF = 256
 
 
-def deal(copy, grouped, raw, c0):
-    m0, n = c0 // PACK, raw.shape[2] // PACK
+def deal(copy, grouped, raw, i):
     copy(
-        grouped[:, :, m0 : m0 + n, :].rearrange("p t m j -> p m j t"),
-        raw.rearrange("p j (m t) -> p m j t", t=PACK),
+        grouped[:].rearrange("p u m j -> p m j u"),
+        raw[:].rearrange("p j (m t) -> p m j t", t=PACK)[:, :, :, 2 * i : 2 * i + 2],
     )
 
 
@@ -44,113 +43,130 @@ def tile_attend_tcweights_o_pl_kernel(tc, tab_words, tab_scales, w1, dw1, gain, 
         nc.vector.memset(bytes_all[:].bitcast(I32), 0)
         nc.gpsimd.memset(warm_in[:], 0.0)
         nc.scalar.activation(warm_out[:], warm_in[:], ACT.Sigmoid)
+        shift = sb("shift", [P, 1], F32)
+        nc.gpsimd.tensor_scalar(shift[:], warm_in[:], 1.0, -math.sqrt(0.5), ALU.mult, ALU.add)
 
-        def load_half(name, w, i):
-            half = sb("%s_raw%d" % (name, i), [P, PACK, HALF], F32)
-            nc.sync.dma_start(half[:], w.rearrange("(p j) c -> p j c", j=PACK)[:, :, i * HALF : (i + 1) * HALF])
-            return half
+        def load_weight(name, w):
+            raw = sb(name, [P, PACK, R], F32)
+            nc.sync.dma_start(raw[:], w.rearrange("(p j) c -> p j c", j=PACK))
+            return raw
 
         gain_sb, rs_sb = sb("gain_sb", [P, PACK], F32), sb("rs_sb", [P, PACK], F32)
         nc.sync.dma_start(list1[:], offs)
         nc.sync.dma_start(words_all[:].bitcast(I32), tab_words[0].bitcast(I32))
-        w1_raw = [load_half("w1", w1, 0)]
-        nc.sync.dma_start(list3[:], offs3)
+        nc.sync.dma_start(gain_sb[:], gain.rearrange("(p t) o -> p (t o)", t=PACK))
         for q in range(4):
             nc.sync.dma_start(bytes_all[32 * q : 32 * q + 4, :].bitcast(I32), tab_scales[0, 4 * q : 4 * q + 4, :].bitcast(I32))
-        w1_raw.append(load_half("w1", w1, 1))
-        dw1_raw = [load_half("dw1", dw1, 0)]
-        nc.sync.dma_start(gain_sb[:], gain.rearrange("(p t) o -> p (t o)", t=PACK))
+        w1_raw = load_weight("w1_raw", w1)
+        nc.sync.dma_start(list3[:], offs3)
         nc.sync.dma_start(list2[:], offs2)
-        dw1_raw.append(load_half("dw1", dw1, 1))
-        wor_raw = sb("wor_raw", [P, PACK, F], F32)
-        nc.sync.dma_start(wor_raw[:], wor.rearrange("(p j) c -> p j c", j=PACK))
         nc.sync.dma_start(rs_sb[:], rs.rearrange("(p t) o -> p (t o)", t=PACK))
+        dw1_raw = load_weight("dw1_raw", dw1)
+        wor_raw = load_weight("wor_raw", wor)
         res_sb = sb("res_sb", [P, PACK, M], F32)
         nc.sync.dma_start(res_sb[:], res.rearrange("(p t) m -> p t m", t=PACK))
+
+        rs2 = sb("rs2", [P, PACK], F32)
+        nc.gpsimd.tensor_scalar(rs2[:], rs_sb[:], -2.0, 0.0, ALU.mult, ALU.add)
+        gain_lo = sb("slot_a", [P, 2], F32)
+        nc.gpsimd.tensor_copy(gain_lo[:], gain_sb[:, 0:2])
 
         tab_w, tab_s = sb("tab_w", [P, J], U16), sb("tab_s", [P, J], U8)
         nc.vector.tensor_copy(tab_w[:], words_all[:].indirect(list1[:]))
         nc.vector.tensor_copy(tab_s[:], bytes_all[:].indirect(list1[:]))
 
-        def operand(name):
-            return sb(name + "_bf", [P, PACK, P, PACK], BF16), sb(name + "_c", [P, PACK, P], U32), sb(name + "_s", [P, PACK, P], U8)
+        def rounded(copy, name, raw, i):
+            grouped = sb(name, [P, 2, P, PACK], BF16)
+            deal(copy, grouped, raw, i)
+            return grouped
 
-        def quantise(op, t0, t1):
-            grouped, codes, scales = op
+        def operand(name):
+            return sb(name + "_c", [P, PACK, P], U32), sb(name + "_s", [P, PACK, P], U8)
+
+        def quantise(op, grouped, t0, t1):
             nc.vector.quantize_mx(
-                out=codes[:, t0:t1, :].rearrange("p t m -> p (t m)").bitcast(FP8X4),
-                scales=scales[:, t0:t1, :].rearrange("p t m -> p (t m)"),
-                in_=grouped[:, t0:t1, :, :].rearrange("p t m j -> p (t m j)"),
+                out=op[0][:, t0:t1, :].rearrange("p t m -> p (t m)").bitcast(FP8X4),
+                scales=op[1][:, t0:t1, :].rearrange("p t m -> p (t m)"),
+                in_=grouped[:, t0 % 2 : t0 % 2 + t1 - t0, :, :].rearrange("p u m j -> p (u m j)"),
             )
 
         def first_layer(op, bank, t):
             nc.tensor.matmul_mx(
-                out=bank[:], lhsT=op[1][:, t, :].bitcast(FP8X4), lhsT_scale=op[2][:, t, :],
+                out=bank[:], lhsT=op[0][:, t, :].bitcast(FP8X4), lhsT_scale=op[1][:, t, :],
                 rhs=tab_w[:].bitcast(FP4X4), rhs_scale=tab_s[:], start=True, stop=True,
             )
 
-        w1q, dw1q, worq = operand("w1"), operand("dw1"), operand("wor")
+        w1q, dw1q = operand("w1"), operand("dw1")
         a_bank = [psum.tile([P, J], F32, name="a%d" % t) for t in range(PACK)]
         ta_bank = [psum.tile([P, J], F32, name="ta%d" % t) for t in range(PACK)]
         h1 = [sb("h1_%d" % t, [P, J], F32) for t in range(PACK)]
         th1 = [sb("th1_%d" % t, [P, J], F32) for t in range(PACK)]
-        s2, s3, tsq, s3r, wb, pa, pb = [sb(n, [P, PACK, M], F32) for n in ("s2", "s3", "tsq", "s3r", "wb", "pa", "pb")]
+        pa, pb = [sb(n, [P, PACK, M], F32) for n in ("pa", "pb")]
 
-        deal(nc.scalar.copy, w1q[0], w1_raw[0][:], 0)
-        deal(nc.vector.tensor_copy, w1q[0], w1_raw[1][:], HALF)
-        for t0, t1 in ((0, 1), (1, 2), (2, 4)):
-            quantise(w1q, t0, t1)
+        w1_lo = rounded(nc.vector.tensor_copy, "w1_lo", w1_raw, 0)
+        w1_hi = rounded(nc.scalar.copy, "w1_hi", w1_raw, 1)
+        quantise(w1q, w1_lo, 0, 1)
+        quantise(w1q, w1_lo, 1, 2)
+        quantise(w1q, w1_hi, 2, 4)
         for t in range(PACK):
             first_layer(w1q, a_bank[t], t)
-        for i in range(2):
-            deal(nc.vector.tensor_copy, dw1q[0], dw1_raw[i][:], i * HALF)
-        for t0, t1 in ((0, 1), (1, 2), (2, 4)):
-            quantise(dw1q, t0, t1)
+        dw1_lo = rounded(nc.vector.tensor_copy, "dw1_lo", dw1_raw, 0)
+        dw1_hi = rounded(nc.vector.tensor_copy, "dw1_hi", dw1_raw, 1)
+        quantise(dw1q, dw1_lo, 0, 2)
+        quantise(dw1q, dw1_hi, 2, 4)
         for t in range(PACK):
             first_layer(dw1q, ta_bank[t], t)
 
         for t in (0, 1):
-            nc.vector.tensor_scalar_mul(th1[t][:], ta_bank[t][:], gain_sb[:, t : t + 1])
-        deal(nc.vector.tensor_copy, worq[0], wor_raw[:], 0)
-        quantise(worq, 0, PACK)
-        n3r, wa = sb("wor_raw", [P, PACK, M], F32), sb("wor_bf", [P, PACK, M], F32)
+            nc.vector.tensor_scalar_mul(th1[t][:], ta_bank[t][:], gain_lo[:, t : t + 1])
 
         for t0 in (0, 2):
-            pair = slice(t0, t0 + 2)
+            s2, s3, tsq, s3r = [sb("%s_%d" % (n, t0), [P, 2, M], F32) for n in ("s2", "s3", "tsq", "s3r")]
             for t in (t0, t0 + 1):
                 nc.scalar.activation(h1[t][:], a_bank[t][:], ACT.Copy, scale=gain_sb[:, t : t + 1])
             for t in (t0, t0 + 1):
-                nc.scalar.activation(s3[:, t, :], h1[t][:].indirect(list3[:]), ACT.Sigmoid)
-                nc.scalar.activation(s2[:, t, :], h1[t][:].indirect(list2[:]), ACT.Sigmoid, scale=2.0)
+                nc.scalar.activation(s3[:, t - t0, :], h1[t][:].indirect(list3[:]), ACT.Sigmoid)
+                nc.scalar.activation(s2[:, t - t0, :], h1[t][:].indirect(list2[:]), ACT.Sigmoid, scale=2.0)
             for t in (t0, t0 + 1):
-                nc.scalar.activation(s3r[:, t, :], s3[:, t, :], ACT.Copy, scale=rs_sb[:, t : t + 1])
-            nc.scalar.activation(tsq[:, pair, :], s2[:, pair, :], ACT.Square, scale=2.0, bias=-1.0)
+                nc.scalar.activation(s3r[:, t - t0, :], s3[:, t - t0, :], ACT.Copy, scale=rs2[:, t : t + 1])
+            nc.scalar.activation(tsq[:], s2[:], ACT.Square, scale=math.sqrt(2.0), bias=shift[:])
             for t in (t0, t0 + 1):
                 if t > 1:
                     nc.scalar.activation(th1[t][:], ta_bank[t][:], ACT.Copy, scale=gain_sb[:, t : t + 1])
-            nc.vector.scalar_tensor_tensor(n3r[:, pair, :], s3[:, pair, :], 1.0, s3r[:, pair, :], ALU.subtract, ALU.mult)
-            nc.vector.scalar_tensor_tensor(wa[:, pair, :], tsq[:, pair, :], 1.0, s3r[:, pair, :], ALU.subtract, ALU.mult)
-            nc.vector.scalar_tensor_tensor(wb[:, pair, :], s2[:, pair, :], 0.5, n3r[:, pair, :], ALU.subtract, ALU.mult)
-            for t in (t0, t0 + 1):
-                nc.vector.tensor_tensor(pa[:, t, :], th1[t][:].indirect(list2[:]), wa[:, t, :], ALU.mult)
-                nc.vector.tensor_tensor(pb[:, t, :], th1[t][:].indirect(list3[:]), wb[:, t, :], ALU.mult)
+            factors, wb = sb("slot_a", [P, 2, 2, M], F32), sb("slot_b", [P, 2, M], F32)[:]
+            n3r, wa = factors[:, 0, :, :], factors[:, 1, :, :]
+            nc.vector.scalar_tensor_tensor(n3r, s3[:], 1.0, s3r[:], ALU.subtract, ALU.mult)
+            nc.vector.scalar_tensor_tensor(wa, tsq[:], 0.5, s3r[:], ALU.subtract, ALU.mult)
+            nc.vector.scalar_tensor_tensor(wb, s2[:], 0.5, n3r, ALU.subtract, ALU.mult)
+            for u in range(2):
+                nc.vector.tensor_tensor(pa[:, t0 + u, :], th1[t0 + u][:].indirect(list2[:]), wa[:, u, :], ALU.mult)
+            for u in range(2):
+                nc.vector.tensor_tensor(pb[:, t0 + u, :], th1[t0 + u][:].indirect(list3[:]), wb[:, u, :], ALU.mult)
 
+        wor_lo = rounded(nc.scalar.copy, "s3r_2", wor_raw, 0)
+        wor_hi = rounded(nc.scalar.copy, "s2_2", wor_raw, 1)
+        worq = [(sb("slot_a", [P, 2, P], U32), sb("wor_lo_s", [P, 2, P], U8))]
+        quantise(worq[0], wor_lo, 0, 2)
         fo_bf, fo_c, fo_s = sb("fo_bf", [P, M, PACK], BF16), sb("fo_c", [P, M], U32), sb("fo_s", [P, M], U8)
-        nc.vector.scalar_tensor_tensor(
-            fo_bf[:], pb[:].rearrange("p t m -> p m t"), -2.0, pa[:].rearrange("p t m -> p m t"), ALU.mult, ALU.subtract
+        nc.vector.tensor_tensor(
+            fo_bf[:].rearrange("p (c i) t -> p c t i", i=4),
+            pa[:].rearrange("p t (c i) -> p c t i", i=4),
+            pb[:].rearrange("p t (c i) -> p c t i", i=4),
+            ALU.add,
         )
+        worq.append((sb("slot_b", [P, 2, P], U32), sb("wor_hi_s", [P, 2, P], U8)))
+        quantise(worq[1], wor_hi, 0, 2)
         nc.vector.quantize_mx(out=fo_c[:].bitcast(FP8X4), scales=fo_s[:], in_=fo_bf[:].rearrange("p m t -> p (m t)"))
 
-        y, y_bf = sb("y", [P, PACK, M], F32), sb("y_bf", [P, M, PACK], BF16)
+        y, y_bf = sb("s2_2", [P, PACK, M], F32), sb("y_bf", [P, M, PACK], BF16)
         y_c, y_s = sb("y_c", [P, M], U32), sb("y_s", [P, M], U8)
         out_rows = out_0.rearrange("(p t) m -> p t m", t=PACK)
         for i in range(2):
             pair = slice(2 * i, 2 * i + 2)
             yo = psum.tile([P, 2, M], F32, name="a%d" % i)
             for u in range(2):
-                t = 2 * i + u
                 nc.tensor.matmul_mx(
-                    out=yo[:, u, :], lhsT=worq[1][:, t, :].bitcast(FP8X4), lhsT_scale=worq[2][:, t, :],
+                    out=yo[:, u, :], lhsT=worq[i][0][:, u, :].bitcast(FP8X4), lhsT_scale=worq[i][1][:, u, :],
                     rhs=fo_c[:].bitcast(FP8X4), rhs_scale=fo_s[:], start=True, stop=True,
                 )
             nc.vector.tensor_tensor(y[:, pair, :], yo[:], res_sb[:, pair, :], ALU.add)

import math
from contextlib import ExitStack

import concourse.mybir as mybir

K, R, F, T, J, M = 512, 512, 512, 2048, 512, 128
FLOPS = 2 * K * R * J * 2 + 2 * R * F * M

F32 = mybir.dt.float32
BF16 = mybir.dt.bfloat16
I32 = mybir.dt.int32
U32 = mybir.dt.uint32
U16 = mybir.dt.uint16
U8 = mybir.dt.uint8
FP8X4 = mybir.dt.float8_e4m3fn_x4
FP4X4 = mybir.dt.float4_e2m1fn_x4
ALU = mybir.AluOpType
ACT = mybir.ActivationFunctionType

P = 128
PACK = 4


def deal(copy, grouped, raw, i):
    copy(
        grouped[:].rearrange("p u m j -> p m j u"),
        raw[:].rearrange("p j (m t) -> p m j t", t=PACK)[:, :, :, 2 * i : 2 * i + 2],
    )


def tile_attend_tcweights_o_pl_kernel(tc, tab_words, tab_scales, w1, dw1, gain, rs, wor, res, offs, offs2, offs3, out_0, out_1, out_2):
    nc = tc.nc
    with ExitStack() as ctx:
        keep = ctx.enter_context(tc.tile_pool(name="keep", bufs=1))
        psum = ctx.enter_context(tc.psum_pool(name="psum", bufs=1))

        def sb(name, shape, dtype):
            return keep.tile(shape, dtype, name=name, align_bytes=64)

        list1, list2, list3 = sb("list1", [P, J // 16], U16), sb("list2", [P, M // 16], U16), sb("list3", [P, M // 16], U16)
        words_all, bytes_all = sb("words_all", [P, T], U16), sb("bytes_all", [P, T], U8)
        warm_in, warm_out = sb("warm_in", [P, 1], F32), sb("warm_out", [P, 1], F32)
        nc.vector.memset(bytes_all[:].bitcast(I32), 0)
        nc.gpsimd.memset(warm_in[:], 0.0)
        nc.scalar.activation(warm_out[:], warm_in[:], ACT.Sigmoid)
        shift = sb("shift", [P, 1], F32)
        nc.gpsimd.tensor_scalar(shift[:], warm_in[:], 1.0, -math.sqrt(0.5), ALU.mult, ALU.add)

        def load_weight(name, w):
            raw = sb(name, [P, PACK, R], F32)
            nc.sync.dma_start(raw[:], w.rearrange("(p j) c -> p j c", j=PACK))
            return raw

        gain_sb, rs_sb = sb("gain_sb", [P, PACK], F32), sb("rs_sb", [P, PACK], F32)
        nc.sync.dma_start(list1[:], offs)
        nc.sync.dma_start(words_all[:].bitcast(I32), tab_words[0].bitcast(I32))
        nc.sync.dma_start(gain_sb[:], gain.rearrange("(p t) o -> p (t o)", t=PACK))
        for q in range(4):
            nc.sync.dma_start(bytes_all[32 * q : 32 * q + 4, :].bitcast(I32), tab_scales[0, 4 * q : 4 * q + 4, :].bitcast(I32))
        w1_raw = load_weight("w1_raw", w1)
        nc.sync.dma_start(list3[:], offs3)
        nc.sync.dma_start(list2[:], offs2)
        nc.sync.dma_start(rs_sb[:], rs.rearrange("(p t) o -> p (t o)", t=PACK))
        dw1_raw = load_weight("dw1_raw", dw1)
        wor_raw = load_weight("wor_raw", wor)
        res_sb = sb("res_sb", [P, PACK, M], F32)
        nc.sync.dma_start(res_sb[:], res.rearrange("(p t) m -> p t m", t=PACK))

        rs2 = sb("rs2", [P, PACK], F32)
        nc.gpsimd.tensor_scalar(rs2[:], rs_sb[:], -2.0, 0.0, ALU.mult, ALU.add)
        gain_lo = sb("slot_a", [P, 2], F32)
        nc.gpsimd.tensor_copy(gain_lo[:], gain_sb[:, 0:2])

        tab_w, tab_s = sb("tab_w", [P, J], U16), sb("tab_s", [P, J], U8)
        nc.vector.tensor_copy(tab_w[:], words_all[:].indirect(list1[:]))
        nc.vector.tensor_copy(tab_s[:], bytes_all[:].indirect(list1[:]))

        def rounded(copy, name, raw, i):
            grouped = sb(name, [P, 2, P, PACK], BF16)
            deal(copy, grouped, raw, i)
            return grouped

        def operand(name):
            return sb(name + "_c", [P, PACK, P], U32), sb(name + "_s", [P, PACK, P], U8)

        def quantise(op, grouped, t0, t1):
            nc.vector.quantize_mx(
                out=op[0][:, t0:t1, :].rearrange("p t m -> p (t m)").bitcast(FP8X4),
                scales=op[1][:, t0:t1, :].rearrange("p t m -> p (t m)"),
                in_=grouped[:, t0 % 2 : t0 % 2 + t1 - t0, :, :].rearrange("p u m j -> p (u m j)"),
            )

        def first_layer(op, bank, t):
            nc.tensor.matmul_mx(
                out=bank[:], lhsT=op[0][:, t, :].bitcast(FP8X4), lhsT_scale=op[1][:, t, :],
                rhs=tab_w[:].bitcast(FP4X4), rhs_scale=tab_s[:], start=True, stop=True,
            )

        w1q, dw1q = operand("w1"), operand("dw1")
        a_bank = [psum.tile([P, J], F32, name="a%d" % t) for t in range(PACK)]
        ta_bank = [psum.tile([P, J], F32, name="ta%d" % t) for t in range(PACK)]
        h1 = [sb("h1_%d" % t, [P, J], F32) for t in range(PACK)]
        th1 = [sb("th1_%d" % t, [P, J], F32) for t in range(PACK)]
        pa, pb = [sb(n, [P, PACK, M], F32) for n in ("pa", "pb")]

        w1_lo = rounded(nc.vector.tensor_copy, "w1_lo", w1_raw, 0)
        w1_hi = rounded(nc.scalar.copy, "w1_hi", w1_raw, 1)
        quantise(w1q, w1_lo, 0, 1)
        quantise(w1q, w1_lo, 1, 2)
        quantise(w1q, w1_hi, 2, 4)
        for t in range(PACK):
            first_layer(w1q, a_bank[t], t)
        dw1_lo = rounded(nc.vector.tensor_copy, "dw1_lo", dw1_raw, 0)
        dw1_hi = rounded(nc.vector.tensor_copy, "dw1_hi", dw1_raw, 1)
        quantise(dw1q, dw1_lo, 0, 2)
        quantise(dw1q, dw1_hi, 2, 4)
        for t in range(PACK):
            first_layer(dw1q, ta_bank[t], t)

        for t in (0, 1):
            nc.vector.tensor_scalar_mul(th1[t][:], ta_bank[t][:], gain_lo[:, t : t + 1])

        for t0 in (0, 2):
            s2, s3, tsq, s3r = [sb("%s_%d" % (n, t0), [P, 2, M], F32) for n in ("s2", "s3", "tsq", "s3r")]
            for t in (t0, t0 + 1):
                nc.scalar.activation(h1[t][:], a_bank[t][:], ACT.Copy, scale=gain_sb[:, t : t + 1])
            for t in (t0, t0 + 1):
                nc.scalar.activation(s3[:, t - t0, :], h1[t][:].indirect(list3[:]), ACT.Sigmoid)
                nc.scalar.activation(s2[:, t - t0, :], h1[t][:].indirect(list2[:]), ACT.Sigmoid, scale=2.0)
            for t in (t0, t0 + 1):
                nc.scalar.activation(s3r[:, t - t0, :], s3[:, t - t0, :], ACT.Copy, scale=rs2[:, t : t + 1])
            nc.scalar.activation(tsq[:], s2[:], ACT.Square, scale=math.sqrt(2.0), bias=shift[:])
            for t in (t0, t0 + 1):
                if t > 1:
                    nc.scalar.activation(th1[t][:], ta_bank[t][:], ACT.Copy, scale=gain_sb[:, t : t + 1])
            factors, wb = sb("slot_a", [P, 2, 2, M], F32), sb("slot_b", [P, 2, M], F32)[:]
            n3r, wa = factors[:, 0, :, :], factors[:, 1, :, :]
            nc.vector.scalar_tensor_tensor(n3r, s3[:], 1.0, s3r[:], ALU.subtract, ALU.mult)
            nc.vector.scalar_tensor_tensor(wa, tsq[:], 0.5, s3r[:], ALU.subtract, ALU.mult)
            nc.vector.scalar_tensor_tensor(wb, s2[:], 0.5, n3r, ALU.subtract, ALU.mult)
            for u in range(2):
                nc.vector.tensor_tensor(pa[:, t0 + u, :], th1[t0 + u][:].indirect(list2[:]), wa[:, u, :], ALU.mult)
            for u in range(2):
                nc.vector.tensor_tensor(pb[:, t0 + u, :], th1[t0 + u][:].indirect(list3[:]), wb[:, u, :], ALU.mult)

        wor_lo = rounded(nc.scalar.copy, "s3r_2", wor_raw, 0)
        wor_hi = rounded(nc.scalar.copy, "s2_2", wor_raw, 1)
        worq = [(sb("slot_a", [P, 2, P], U32), sb("wor_lo_s", [P, 2, P], U8))]
        quantise(worq[0], wor_lo, 0, 2)
        fo_bf, fo_c, fo_s = sb("fo_bf", [P, M, PACK], BF16), sb("fo_c", [P, M], U32), sb("fo_s", [P, M], U8)
        nc.vector.tensor_tensor(
            fo_bf[:].rearrange("p (c i) t -> p c t i", i=4),
            pa[:].rearrange("p t (c i) -> p c t i", i=4),
            pb[:].rearrange("p t (c i) -> p c t i", i=4),
            ALU.add,
        )
        worq.append((sb("slot_b", [P, 2, P], U32), sb("wor_hi_s", [P, 2, P], U8)))
        quantise(worq[1], wor_hi, 0, 2)
        nc.vector.quantize_mx(out=fo_c[:].bitcast(FP8X4), scales=fo_s[:], in_=fo_bf[:].rearrange("p m t -> p (m t)"))

        y, y_bf = sb("s2_2", [P, PACK, M], F32), sb("y_bf", [P, M, PACK], BF16)
        y_c, y_s = sb("y_c", [P, M], U32), sb("y_s", [P, M], U8)
        out_rows = out_0.rearrange("(p t) m -> p t m", t=PACK)
        for i in range(2):
            pair = slice(2 * i, 2 * i + 2)
            yo = psum.tile([P, 2, M], F32, name="a%d" % i)
            for u in range(2):
                nc.tensor.matmul_mx(
                    out=yo[:, u, :], lhsT=worq[i][0][:, u, :].bitcast(FP8X4), lhsT_scale=worq[i][1][:, u, :],
                    rhs=fo_c[:].bitcast(FP8X4), rhs_scale=fo_s[:], start=True, stop=True,
                )
            nc.vector.tensor_tensor(y[:, pair, :], yo[:], res_sb[:, pair, :], ALU.add)
            nc.sync.dma_start(out_rows[:, pair, :], y[:, pair, :])
        nc.vector.tensor_copy(y_bf[:].rearrange("p (c i) t -> p c t i", i=4), y[:].rearrange("p t (c i) -> p c t i", i=4))
        nc.vector.quantize_mx(out=y_c[:].bitcast(FP8X4), scales=y_s[:], in_=y_bf[:].rearrange("p m t -> p (m t)"))
        nc.scalar.dma_start(out_1[0].rearrange("p c r -> p (c r)").bitcast(I32), y_c[:].bitcast(I32))
        for q in range(4):
            queue = nc.sync if q % 2 == 0 else nc.scalar
            queue.dma_start(out_2[0, 4 * q : 4 * q + 4, :].bitcast(I32), y_s[32 * q : 32 * q + 4, :].bitcast(I32))
